import numpy as np
import ml_dtypes


def mxq(x, axis, fmt="e4m3"):
    dtype, down = {"e4m3": (ml_dtypes.float8_e4m3fn, 7), "e5m2": (ml_dtypes.float8_e5m2, 14)}[fmt]
    v = np.moveaxis(np.asarray(x, np.float32).astype(ml_dtypes.bfloat16).astype(np.float64), axis, -1)
    blocks = v.reshape(v.shape[:-1] + (-1, 32))
    amax = np.abs(blocks).max(-1, keepdims=True)
    byte = np.maximum(np.where(amax > 0, np.frexp(amax)[1] - 1 + 127, 0) - down, 1)
    scale = np.exp2(byte - 127.0)
    codes = (blocks / scale).astype(np.float32).astype(dtype).astype(np.float64)
    return np.moveaxis((codes * scale).reshape(v.shape), -1, axis)


WIDE = False


def mx_kscale(k):
    if not WIDE:
        return np.ones(k)
    levels = np.array([30, -30])
    if k % 512:
        return np.exp2(np.random.permutation(np.resize(levels, k // 32))).repeat(32)
    a = np.empty((k // 512, 16))
    for p in range(k // 512):
        a[p, :8] = np.random.permutation(np.resize(levels, 8))
        for g in range(8):
            far = levels[np.abs(levels - a[p, g]) >= 10]
            a[p, g + 8] = far[np.random.randint(len(far))]
    return np.exp2(a.ravel()).repeat(32)


def f64(x):
    return np.asarray(x).astype(np.float64)


def striped(idx):
    return np.tile(np.asarray(idx).reshape(-1, 16).T, (8, 1)).astype(np.uint16)


def unstriped(offs):
    return offs[:16].T.reshape(-1).astype(np.int64)


E2M1 = np.array([0.0, 0.5, 1.0, 1.5, 2.0, 3.0, 4.0, 6.0, -0.0, -0.5, -1.0, -1.5, -2.0, -3.0, -4.0, -6.0])


def pack_weight(w, fmt):
    k, n = w.shape
    w = f64(np.asarray(w, np.float32).astype(ml_dtypes.bfloat16)).reshape(k // 32, 32, n)
    amax = np.abs(w).max(1)
    if fmt == "e4m3":
        byte = np.frexp(amax)[1] - 1 + 127 - 7
    else:
        mant, ex = np.frexp(amax / 6.0)
        byte = np.where(mant > 0.5, ex, ex - 1) + 127
    byte = np.clip(np.where(amax > 0, byte, 1), 1, 254)
    scaled = (w * np.exp2(127.0 - byte)[:, None, :]).reshape(k, n).astype(np.float32)
    by_word = np.ascontiguousarray(scaled.reshape(k // 512, 128, 4, n).transpose(0, 1, 3, 2))
    if fmt == "e4m3":
        words = by_word.astype(ml_dtypes.float8_e4m3fn).view(np.uint8)
    else:
        c = by_word.astype(ml_dtypes.float4_e2m1fn).view(np.uint8) & 0xF
        words = (c[..., 0::2] | (c[..., 1::2] << 4)).reshape(k // 512, 128, 2 * n)
    return np.ascontiguousarray(words), np.ascontiguousarray(byte.astype(np.uint8).reshape(k // 512, 16, n))


def unpack_weight(words, scales, fmt):
    g, _, n = scales.shape
    words = np.ascontiguousarray(words).reshape(g, 128, n, -1)
    if fmt == "e4m3":
        vals = words.view(ml_dtypes.float8_e4m3fn).astype(np.float64)
    else:
        nib = np.empty((g, 128, n, 4), np.uint8)
        nib[..., 0::2] = words & 0xF
        nib[..., 1::2] = words >> 4
        vals = E2M1[nib]
    vals = vals * np.repeat(np.exp2(scales.astype(np.float64) - 127.0), 8, axis=1)[..., None]
    return vals.transpose(0, 1, 3, 2).reshape(g * 512, n)


K, T, J, I, L = 1024, 1024, 256, 256, 512


def setup_inputs():
    n = np.random.standard_normal
    idx = np.random.permutation(T)[:J]
    fk = mx_kscale(K)
    fl = mx_kscale(L)
    xtp = pack_weight(n((K, T)) * 0.04 * fk[:, None], "e4m3")
    cxp = pack_weight(n((L, J)) / fl[:, None], "e2m1")
    wcp = pack_weight(n((L, I)) * 1 / np.sqrt(L) * fl[:, None], "e4m3")
    return {
        "xt_words": xtp[0],
        "xt_scales": xtp[1],
        "ky": (n((K, I)) / fk[:, None]).astype(np.float32),
        "bi": (np.random.uniform(-0.7, 0.7, (1, I))).astype(np.float32),
        "cx_words": cxp[0],
        "cx_scales": cxp[1],
        "wc_words": wcp[0],
        "wc_scales": wcp[1],
        "offs": striped(idx),
    }


def reference(xt_words, xt_scales, ky, bi, cx_words, cx_scales, wc_words, wc_scales, offs):
    idx = unstriped(offs)
    xtu = unpack_weight(xt_words, xt_scales, "e4m3")
    cxu = unpack_weight(cx_words, cx_scales, "e2m1")
    wcu = unpack_weight(wc_words, wc_scales, "e4m3")
    xtidxg = xtu[:, idx]
    kyq = mxq(f64(ky), 0, "e5m2")
    a0 = xtidxg.T @ kyq
    a = a0 + f64(bi)
    q = cxu.T @ wcu
    y = np.maximum(a, q) - 0.5 * np.minimum(a, q)
    return y

@@ -1,0 +1,159 @@
+from contextlib import ExitStack
+
+import concourse.mybir as mybir
+from concourse.masks import make_identity
+
+K, T, J, I, L = 1024, 1024, 256, 256, 512
+FLOPS = 2 * J * I * (K + L)
+
+F32 = mybir.dt.float32
+BF16 = mybir.dt.bfloat16
+I32 = mybir.dt.int32
+U32 = mybir.dt.uint32
+U16 = mybir.dt.uint16
+U8 = mybir.dt.uint8
+E4M3 = mybir.dt.float8_e4m3fn_x4
+E5M2 = mybir.dt.float8_e5m2_x4
+E2M1 = mybir.dt.float4_e2m1fn_x4
+ALU = mybir.AluOpType
+
+P = 128
+PACK = 4
+K_PASS = P * PACK
+PASSES = K // K_PASS
+ROW_TILES = J // P
+QUAD = 32
+LIST_COLS = P // 16
+
+
+def tile_list_scores_picked_given_tworank_kernel(
+    tc, xt_words, xt_scales, ky, bi, cx_words, cx_scales, wc_words, wc_scales, offs, out
+):
+    nc = tc.nc
+    with ExitStack() as ctx:
+        sb = ctx.enter_context(tc.tile_pool(name="sb", bufs=1))
+        ps = ctx.enter_context(tc.psum_pool(name="ps", bufs=1))
+
+        offsets = sb.tile([P, J // 16], U16, name="offsets")
+        xt_w = [sb.tile([P, T], I32, name=f"xt_w{z}", align_bytes=64) for z in range(PASSES)]
+        xt_s = sb.tile([P, PASSES, T // 4], I32, name="xt_s", align_bytes=64)
+        ky_raw = [sb.tile([P, PACK, I], F32, name=f"ky_raw{z}", align_bytes=64) for z in range(PASSES)]
+        ky_bf = [sb.tile([P, I, PACK], BF16, name=f"ky_bf{z}", align_bytes=64) for z in range(PASSES)]
+        ky_w = [sb.tile([P, I], U32, name=f"ky_w{z}", align_bytes=64) for z in range(PASSES)]
+        ky_s = [sb.tile([P, I], U8, name=f"ky_s{z}", align_bytes=64) for z in range(PASSES)]
+        pick_w = [sb.tile([P, J], U32, name=f"pick_w{z}", align_bytes=64) for z in range(PASSES)]
+        pick_s = [sb.tile([P, J], U8, name=f"pick_s{z}", align_bytes=64) for z in range(PASSES)]
+        cx_w = sb.tile([P, J // 2], I32, name="cx_w", align_bytes=64)
+        wc_w = sb.tile([P, I], I32, name="wc_w", align_bytes=64)
+        cx_s = sb.tile([P, J // 4], I32, name="cx_s", align_bytes=64)
+        wc_s = sb.tile([P, I // 4], I32, name="wc_s", align_bytes=64)
+        bias_pairs = sb.tile([P, 2], F32, name="bias_pairs")
+        bias = sb.tile([P, I], F32, name="bias")
+        ident = sb.tile([P, P], F32, name="ident")
+        q_less_bias = sb.tile([P, ROW_TILES, I], F32, name="q_less_bias")
+        diff = [sb.tile([P, I], F32, name=f"diff{r}") for r in range(ROW_TILES)]
+        kept = [sb.tile([P, I], F32, name=f"kept{r}") for r in range(ROW_TILES)]
+        res = [sb.tile([P, I], F32, name=f"res{r}") for r in range(ROW_TILES)]
+
+        bias_ps = ps.tile([P, 2, P], F32, name="bias_ps")
+        q_ps = ps.tile([P, ROW_TILES, I], F32, name="q_ps")
+        a0_ps = [ps.tile([P, I], F32, name=f"a0_ps{r}") for r in range(ROW_TILES)]
+
+        def load_scale_rows(queue, plane, scales, r):
+            rows = scales.bitcast(I32).rearrange("z (q r) c -> r q z c", r=4)[r]
+            queue.dma_start(out=plane[r:P:QUAD], in_=rows)
+
+        def load_ky(z):
+            rows = ky[z * K_PASS : (z + 1) * K_PASS, :]
+            nc.sync.dma_start(out=ky_raw[z][:], in_=rows.rearrange("(p t) i -> p t i", t=PACK))
+
+        def load_xt_words(z):
+            nc.sync.dma_start(out=xt_w[z][:], in_=xt_words[z].rearrange("p n t -> p (n t)").bitcast(I32))
+
+        nc.vector.memset(xt_s[:], 0)
+        nc.vector.memset(cx_s[:], 0)
+        nc.vector.memset(wc_s[:], 0)
+
+        load_ky(0)
+        for r in range(4):
+            load_scale_rows(nc.scalar, xt_s[:], xt_scales, r)
+        nc.sync.dma_start(offsets[:], offs)
+        load_ky(1)
+        nc.sync.dma_start(out=bias_pairs[:], in_=bi.rearrange("o (p c) -> p (o c)", c=2))
+        load_xt_words(0)
+        nc.sync.dma_start(out=cx_w[:], in_=cx_words[0].bitcast(I32))
+        nc.sync.dma_start(out=wc_w[:], in_=wc_words[0].rearrange("p n t -> p (n t)").bitcast(I32))
+        for r in range(4):
+            load_scale_rows(nc.sync, cx_s[:].unsqueeze(1), cx_scales, r)
+        load_xt_words(1)
+        make_identity(nc, ident[:])
+        for r in range(4):
+            load_scale_rows(nc.gpsimd, wc_s[:].unsqueeze(1), wc_scales, r)
+
+        def gather(dst, window, dtype, cols):
+            nc.vector.tensor_copy(dst, window.bitcast(dtype).indirect(offsets[:, cols]))
+
+        def weave_ky(z):
+            nc.scalar.copy(
+                out=ky_bf[z][:].rearrange("p (c n) t -> p c t n", n=4),
+                in_=ky_raw[z][:].rearrange("p t (c n) -> p c t n", n=4),
+            )
+
+        def quantize_ky(z):
+            nc.vector.quantize_mx(
+                out=ky_w[z][:].bitcast(E5M2), scales=ky_s[z][:], in_=ky_bf[z][:].rearrange("p i t -> p (i t)")
+            )
+
+        def score_pass(z, r):
+            rows = slice(r * P, (r + 1) * P)
+            nc.tensor.matmul_mx(
+                out=a0_ps[r][:],
+                lhsT=pick_w[z][:, rows].bitcast(E4M3),
+                lhsT_scale=pick_s[z][:, rows],
+                rhs=ky_w[z][:].bitcast(E5M2),
+                rhs_scale=ky_s[z][:],
+                start=(z == 0),
+                stop=(z == PASSES - 1),
+            )
+
+        whole_list = slice(0, J // 16)
+        weave_ky(0)
+        for z in range(PASSES):
+            gather(pick_s[z][:], xt_s[:, z, :], U8, whole_list)
+        quantize_ky(0)
+        weave_ky(1)
+
+        for c in range(2):
+            nc.tensor.transpose(bias_ps[:, c, :], bias_pairs[:, c : c + 1].to_broadcast([P, P]), ident[:])
+        nc.scalar.copy(out=bias[:].rearrange("p (n c) -> p n c", c=2), in_=bias_ps[:].rearrange("p c n -> p n c"))
+
+        gather(pick_w[0][:], xt_w[0][:], U32, whole_list)
+        quantize_ky(1)
+        for r in range(ROW_TILES):
+            score_pass(0, r)
+
+        for r in range(ROW_TILES):
+            nc.tensor.matmul_mx(
+                out=q_ps[:, r, :],
+                lhsT=cx_w[:, r * P // 2 : (r + 1) * P // 2].bitcast(E2M1),
+                lhsT_scale=cx_s[:].bitcast(U8)[:, r * P : (r + 1) * P],
+                rhs=wc_w[:].bitcast(E4M3),
+                rhs_scale=wc_s[:].bitcast(U8),
+                start=True,
+                stop=True,
+            )
+        nc.vector.tensor_tensor(
+            q_less_bias[:], q_ps[:], bias[:].unsqueeze(1).to_broadcast([P, ROW_TILES, I]), ALU.subtract
+        )
+
+        for r in range(ROW_TILES):
+            gather(pick_w[1][:, r * P : (r + 1) * P], xt_w[1][:], U32, slice(r * LIST_COLS, (r + 1) * LIST_COLS))
+            score_pass(1, r)
+
+        for r in range(ROW_TILES):
+            nc.vector.tensor_tensor(diff[r][:], a0_ps[r][:], q_less_bias[:, r, :], ALU.subtract)
+        for r in range(ROW_TILES):
+            nc.vector.scalar_tensor_tensor(kept[r][:], diff[r][:], -0.5, diff[r][:], ALU.mult, ALU.max)
+        for r in range(ROW_TILES):
+            nc.vector.scalar_tensor_tensor(res[r][:], q_ps[:, r, :], 0.5, kept[r][:], ALU.mult, ALU.add)
+            (nc.sync, nc.scalar)[r].dma_start(out=out[r * P : (r + 1) * P, :], in_=res[r][:])

@@ -50,14 +50,13 @@ def tile_list_scores_picked_given_tworank_kernel(
         bias_pairs = sb.tile([P, 2], F32, name="bias_pairs")
         bias = sb.tile([P, I], F32, name="bias")
         ident = sb.tile([P, P], F32, name="ident")
-        q_less_bias = sb.tile([P, ROW_TILES, I], F32, name="q_less_bias")
+        score = [sb.tile([P, I], F32, name=f"score{r}") for r in range(ROW_TILES)]
         diff = [sb.tile([P, I], F32, name=f"diff{r}") for r in range(ROW_TILES)]
         kept = [sb.tile([P, I], F32, name=f"kept{r}") for r in range(ROW_TILES)]
         res = [sb.tile([P, I], F32, name=f"res{r}") for r in range(ROW_TILES)]
 
-        bias_ps = ps.tile([P, 2, P], F32, name="bias_ps")
-        q_ps = ps.tile([P, ROW_TILES, I], F32, name="q_ps")
-        a0_ps = [ps.tile([P, I], F32, name=f"a0_ps{r}") for r in range(ROW_TILES)]
+        bias_ps = ps.tile([P, 2, P], F32, name="bias_ps", tag="bank0")
+        q_ps = [ps.tile([P, I], F32, name=f"q_ps{r}") for r in range(ROW_TILES)]
 
         def load_scale_rows(queue, plane, scales, r):
             rows = scales.bitcast(I32).rearrange("z (q r) c -> r q z c", r=4)[r]
@@ -71,24 +70,26 @@ def tile_list_scores_picked_given_tworank_kernel(
             nc.sync.dma_start(out=xt_w[z][:], in_=xt_words[z].rearrange("p n t -> p (n t)").bitcast(I32))
 
         nc.vector.memset(xt_s[:], 0)
-        nc.vector.memset(cx_s[:], 0)
+        nc.vector.memset(ident[:], 0.0)
         nc.vector.memset(wc_s[:], 0)
+        nc.vector.memset(cx_s[:], 0)
+
+        nc.gpsimd.dma_start(out=bias_pairs[:], in_=bi.rearrange("o (p c) -> p (o c)", c=2))
+        make_identity(nc, ident[:], nomemset=True)
+        for r in range(4):
+            load_scale_rows(nc.gpsimd, wc_s[:].unsqueeze(1), wc_scales, r)
 
         load_ky(0)
         for r in range(4):
-            load_scale_rows(nc.scalar, xt_s[:], xt_scales, r)
+            load_scale_rows(nc.sync, xt_s[:], xt_scales, r)
         nc.sync.dma_start(offsets[:], offs)
         load_ky(1)
-        nc.sync.dma_start(out=bias_pairs[:], in_=bi.rearrange("o (p c) -> p (o c)", c=2))
         load_xt_words(0)
+        load_xt_words(1)
         nc.sync.dma_start(out=cx_w[:], in_=cx_words[0].bitcast(I32))
         nc.sync.dma_start(out=wc_w[:], in_=wc_words[0].rearrange("p n t -> p (n t)").bitcast(I32))
         for r in range(4):
             load_scale_rows(nc.sync, cx_s[:].unsqueeze(1), cx_scales, r)
-        load_xt_words(1)
-        make_identity(nc, ident[:])
-        for r in range(4):
-            load_scale_rows(nc.gpsimd, wc_s[:].unsqueeze(1), wc_scales, r)
 
         def gather(dst, window, dtype, cols):
             nc.vector.tensor_copy(dst, window.bitcast(dtype).indirect(offsets[:, cols]))
@@ -127,14 +128,19 @@ def tile_list_scores_picked_given_tworank_kernel(
             nc.tensor.transpose(bias_ps[:, c, :], bias_pairs[:, c : c + 1].to_broadcast([P, P]), ident[:])
         nc.scalar.copy(out=bias[:].rearrange("p (n c) -> p n c", c=2), in_=bias_ps[:].rearrange("p c n -> p n c"))
 
+        a0_ps = [ps.tile([P, I], F32, name=f"a0_ps{r}", tag=f"bank{r}") for r in range(ROW_TILES)]
         gather(pick_w[0][:], xt_w[0][:], U32, whole_list)
         quantize_ky(1)
         for r in range(ROW_TILES):
             score_pass(0, r)
 
         for r in range(ROW_TILES):
+            gather(pick_w[1][:, r * P : (r + 1) * P], xt_w[1][:], U32, slice(r * LIST_COLS, (r + 1) * LIST_COLS))
+            score_pass(1, r)
+
+        for r in range(ROW_TILES):
             nc.tensor.matmul_mx(
-                out=q_ps[:, r, :],
+                out=q_ps[r][:],
                 lhsT=cx_w[:, r * P // 2 : (r + 1) * P // 2].bitcast(E2M1),
                 lhsT_scale=cx_s[:].bitcast(U8)[:, r * P : (r + 1) * P],
                 rhs=wc_w[:].bitcast(E4M3),
@@ -142,18 +148,13 @@ def tile_list_scores_picked_given_tworank_kernel(
                 start=True,
                 stop=True,
             )
-        nc.vector.tensor_tensor(
-            q_less_bias[:], q_ps[:], bias[:].unsqueeze(1).to_broadcast([P, ROW_TILES, I]), ALU.subtract
-        )
 
         for r in range(ROW_TILES):
-            gather(pick_w[1][:, r * P : (r + 1) * P], xt_w[1][:], U32, slice(r * LIST_COLS, (r + 1) * LIST_COLS))
-            score_pass(1, r)
-
+            nc.vector.tensor_tensor(score[r][:], a0_ps[r][:], bias[:], ALU.add)
         for r in range(ROW_TILES):
-            nc.vector.tensor_tensor(diff[r][:], a0_ps[r][:], q_less_bias[:, r, :], ALU.subtract)
+            nc.vector.tensor_tensor(diff[r][:], q_ps[r][:], score[r][:], ALU.subtract)
         for r in range(ROW_TILES):
             nc.vector.scalar_tensor_tensor(kept[r][:], diff[r][:], -0.5, diff[r][:], ALU.mult, ALU.max)
         for r in range(ROW_TILES):
-            nc.vector.scalar_tensor_tensor(res[r][:], q_ps[:, r, :], 0.5, kept[r][:], ALU.mult, ALU.add)
+            nc.vector.scalar_tensor_tensor(res[r][:], score[r][:], 0.5, kept[r][:], ALU.mult, ALU.add)
             (nc.sync, nc.scalar)[r].dma_start(out=out[r * P : (r + 1) * P, :], in_=res[r][:])

@@ -35,11 +35,10 @@ def tile_list_scores_picked_given_tworank_kernel(
         ps = ctx.enter_context(tc.psum_pool(name="ps", bufs=1))
 
         offsets = sb.tile([P, J // 16], U16, name="offsets")
-        xt_w = [sb.tile([P, T], I32, name=f"xt_w{z}", align_bytes=64) for z in range(PASSES)]
-        xt_s = sb.tile([P, PASSES, T // 4], I32, name="xt_s", align_bytes=64)
+        xt_w = [sb.tile([P, T], I32, name=f"xt_w{z}", tag=f"xt_w{z}", align_bytes=64) for z in range(PASSES)]
+        xt_s = sb.tile([P, PASSES, T // 4], I32, name="xt_s", tag="xt_s", align_bytes=64)
         ky_raw = [sb.tile([P, PACK, I], F32, name=f"ky_raw{z}", align_bytes=64) for z in range(PASSES)]
         ky_bf = [sb.tile([P, I, PACK], BF16, name=f"ky_bf{z}", align_bytes=64) for z in range(PASSES)]
-        ky_w = [sb.tile([P, I], U32, name=f"ky_w{z}", align_bytes=64) for z in range(PASSES)]
         ky_s = [sb.tile([P, I], U8, name=f"ky_s{z}", align_bytes=64) for z in range(PASSES)]
         pick_w = [sb.tile([P, J], U32, name=f"pick_w{z}", align_bytes=64) for z in range(PASSES)]
         pick_s = [sb.tile([P, J], U8, name=f"pick_s{z}", align_bytes=64) for z in range(PASSES)]
@@ -70,19 +69,18 @@ def tile_list_scores_picked_given_tworank_kernel(
             nc.sync.dma_start(out=xt_w[z][:], in_=xt_words[z].rearrange("p n t -> p (n t)").bitcast(I32))
 
         nc.vector.memset(xt_s[:], 0)
-        nc.vector.memset(ident[:], 0.0)
         nc.vector.memset(wc_s[:], 0)
         nc.vector.memset(cx_s[:], 0)
 
-        nc.gpsimd.dma_start(out=bias_pairs[:], in_=bi.rearrange("o (p c) -> p (o c)", c=2))
-        make_identity(nc, ident[:], nomemset=True)
+        nc.scalar.dma_start(out=bias_pairs[:], in_=bi.rearrange("o (p c) -> p (o c)", c=2))
+        make_identity(nc, ident[:])
         for r in range(4):
             load_scale_rows(nc.gpsimd, wc_s[:].unsqueeze(1), wc_scales, r)
 
+        nc.sync.dma_start(offsets[:], offs)
         load_ky(0)
         for r in range(4):
             load_scale_rows(nc.sync, xt_s[:], xt_scales, r)
-        nc.sync.dma_start(offsets[:], offs)
         load_ky(1)
         load_xt_words(0)
         load_xt_words(1)
@@ -121,6 +119,7 @@ def tile_list_scores_picked_given_tworank_kernel(
         weave_ky(0)
         for z in range(PASSES):
             gather(pick_s[z][:], xt_s[:, z, :], U8, whole_list)
+        ky_w = [sb.tile([P, I], U32, name="ky_w0", tag="xt_s", align_bytes=64)]
         quantize_ky(0)
         weave_ky(1)
 
@@ -130,6 +129,7 @@ def tile_list_scores_picked_given_tworank_kernel(
 
         a0_ps = [ps.tile([P, I], F32, name=f"a0_ps{r}", tag=f"bank{r}") for r in range(ROW_TILES)]
         gather(pick_w[0][:], xt_w[0][:], U32, whole_list)
+        ky_w.append(sb.tile([P, I], U32, name="ky_w1", tag="xt_w0", align_bytes=64))
         quantize_ky(1)
         for r in range(ROW_TILES):
             score_pass(0, r)

@@ -68,26 +68,28 @@ def tile_list_scores_picked_given_tworank_kernel(
         def load_xt_words(z):
             nc.sync.dma_start(out=xt_w[z][:], in_=xt_words[z].rearrange("p n t -> p (n t)").bitcast(I32))
 
-        nc.vector.memset(xt_s[:], 0)
         nc.vector.memset(wc_s[:], 0)
+        nc.vector.memset(xt_s[:], 0)
         nc.vector.memset(cx_s[:], 0)
 
         nc.scalar.dma_start(out=bias_pairs[:], in_=bi.rearrange("o (p c) -> p (o c)", c=2))
-        make_identity(nc, ident[:])
-        for r in range(4):
+        for r in range(3):
             load_scale_rows(nc.gpsimd, wc_s[:].unsqueeze(1), wc_scales, r)
+        make_identity(nc, ident[:])
 
         nc.sync.dma_start(offsets[:], offs)
         load_ky(0)
         for r in range(4):
             load_scale_rows(nc.sync, xt_s[:], xt_scales, r)
         load_ky(1)
+        load_scale_rows(nc.sync, cx_s[:].unsqueeze(1), cx_scales, 0)
         load_xt_words(0)
         load_xt_words(1)
         nc.sync.dma_start(out=cx_w[:], in_=cx_words[0].bitcast(I32))
         nc.sync.dma_start(out=wc_w[:], in_=wc_words[0].rearrange("p n t -> p (n t)").bitcast(I32))
-        for r in range(4):
+        for r in range(1, 4):
             load_scale_rows(nc.sync, cx_s[:].unsqueeze(1), cx_scales, r)
+        load_scale_rows(nc.sync, wc_s[:].unsqueeze(1), wc_scales, 3)
 
         def gather(dst, window, dtype, cols):
             nc.vector.tensor_copy(dst, window.bitcast(dtype).indirect(offsets[:, cols]))

from contextlib import ExitStack

import concourse.mybir as mybir
from concourse.masks import make_identity

K, T, J, I, L = 1024, 1024, 256, 256, 512
FLOPS = 2 * J * I * (K + L)

F32 = mybir.dt.float32
BF16 = mybir.dt.bfloat16
I32 = mybir.dt.int32
U32 = mybir.dt.uint32
U16 = mybir.dt.uint16
U8 = mybir.dt.uint8
E4M3 = mybir.dt.float8_e4m3fn_x4
E5M2 = mybir.dt.float8_e5m2_x4
E2M1 = mybir.dt.float4_e2m1fn_x4
ALU = mybir.AluOpType

P = 128
PACK = 4
K_PASS = P * PACK
PASSES = K // K_PASS
ROW_TILES = J // P
QUAD = 32
LIST_COLS = P // 16


def tile_list_scores_picked_given_tworank_kernel(
    tc, xt_words, xt_scales, ky, bi, cx_words, cx_scales, wc_words, wc_scales, offs, out
):
    nc = tc.nc
    with ExitStack() as ctx:
        sb = ctx.enter_context(tc.tile_pool(name="sb", bufs=1))
        ps = ctx.enter_context(tc.psum_pool(name="ps", bufs=1))

        offsets = sb.tile([P, J // 16], U16, name="offsets")
        xt_w = [sb.tile([P, T], I32, name=f"xt_w{z}", tag=f"xt_w{z}", align_bytes=64) for z in range(PASSES)]
        xt_s = sb.tile([P, PASSES, T // 4], I32, name="xt_s", tag="xt_s", align_bytes=64)
        ky_raw = [sb.tile([P, PACK, I], F32, name=f"ky_raw{z}", align_bytes=64) for z in range(PASSES)]
        ky_bf = [sb.tile([P, I, PACK], BF16, name=f"ky_bf{z}", align_bytes=64) for z in range(PASSES)]
        ky_s = [sb.tile([P, I], U8, name=f"ky_s{z}", align_bytes=64) for z in range(PASSES)]
        pick_w = [sb.tile([P, J], U32, name=f"pick_w{z}", align_bytes=64) for z in range(PASSES)]
        pick_s = [sb.tile([P, J], U8, name=f"pick_s{z}", align_bytes=64) for z in range(PASSES)]
        cx_w = sb.tile([P, J // 2], I32, name="cx_w", align_bytes=64)
        wc_w = sb.tile([P, I], I32, name="wc_w", align_bytes=64)
        cx_s = sb.tile([P, J // 4], I32, name="cx_s", align_bytes=64)
        wc_s = sb.tile([P, I // 4], I32, name="wc_s", align_bytes=64)
        bias_pairs = sb.tile([P, 2], F32, name="bias_pairs")
        bias = sb.tile([P, I], F32, name="bias")
        ident = sb.tile([P, P], F32, name="ident")
        score = [sb.tile([P, I], F32, name=f"score{r}") for r in range(ROW_TILES)]
        diff = [sb.tile([P, I], F32, name=f"diff{r}") for r in range(ROW_TILES)]
        kept = [sb.tile([P, I], F32, name=f"kept{r}") for r in range(ROW_TILES)]
        res = [sb.tile([P, I], F32, name=f"res{r}") for r in range(ROW_TILES)]

        bias_ps = ps.tile([P, 2, P], F32, name="bias_ps", tag="bank0")
        q_ps = [ps.tile([P, I], F32, name=f"q_ps{r}") for r in range(ROW_TILES)]

        def load_scale_rows(queue, plane, scales, r):
            rows = scales.bitcast(I32).rearrange("z (q r) c -> r q z c", r=4)[r]
            queue.dma_start(out=plane[r:P:QUAD], in_=rows)

        def load_ky(z):
            rows = ky[z * K_PASS : (z + 1) * K_PASS, :]
            nc.sync.dma_start(out=ky_raw[z][:], in_=rows.rearrange("(p t) i -> p t i", t=PACK))

        def load_xt_words(z):
            nc.sync.dma_start(out=xt_w[z][:], in_=xt_words[z].rearrange("p n t -> p (n t)").bitcast(I32))

        nc.vector.memset(wc_s[:], 0)
        nc.vector.memset(xt_s[:], 0)
        nc.vector.memset(cx_s[:], 0)

        nc.scalar.dma_start(out=bias_pairs[:], in_=bi.rearrange("o (p c) -> p (o c)", c=2))
        for r in range(3):
            load_scale_rows(nc.gpsimd, wc_s[:].unsqueeze(1), wc_scales, r)
        make_identity(nc, ident[:])

        nc.sync.dma_start(offsets[:], offs)
        load_ky(0)
        for r in range(4):
            load_scale_rows(nc.sync, xt_s[:], xt_scales, r)
        load_ky(1)
        load_scale_rows(nc.sync, cx_s[:].unsqueeze(1), cx_scales, 0)
        load_xt_words(0)
        load_xt_words(1)
        nc.sync.dma_start(out=cx_w[:], in_=cx_words[0].bitcast(I32))
        nc.sync.dma_start(out=wc_w[:], in_=wc_words[0].rearrange("p n t -> p (n t)").bitcast(I32))
        for r in range(1, 4):
            load_scale_rows(nc.sync, cx_s[:].unsqueeze(1), cx_scales, r)
        load_scale_rows(nc.sync, wc_s[:].unsqueeze(1), wc_scales, 3)

        def gather(dst, window, dtype, cols):
            nc.vector.tensor_copy(dst, window.bitcast(dtype).indirect(offsets[:, cols]))

        def weave_ky(z):
            nc.scalar.copy(
                out=ky_bf[z][:].rearrange("p (c n) t -> p c t n", n=4),
                in_=ky_raw[z][:].rearrange("p t (c n) -> p c t n", n=4),
            )

        def quantize_ky(z):
            nc.vector.quantize_mx(
                out=ky_w[z][:].bitcast(E5M2), scales=ky_s[z][:], in_=ky_bf[z][:].rearrange("p i t -> p (i t)")
            )

        def score_pass(z, r):
            rows = slice(r * P, (r + 1) * P)
            nc.tensor.matmul_mx(
                out=a0_ps[r][:],
                lhsT=pick_w[z][:, rows].bitcast(E4M3),
                lhsT_scale=pick_s[z][:, rows],
                rhs=ky_w[z][:].bitcast(E5M2),
                rhs_scale=ky_s[z][:],
                start=(z == 0),
                stop=(z == PASSES - 1),
            )

        whole_list = slice(0, J // 16)
        weave_ky(0)
        for z in range(PASSES):
            gather(pick_s[z][:], xt_s[:, z, :], U8, whole_list)
        ky_w = [sb.tile([P, I], U32, name="ky_w0", tag="xt_s", align_bytes=64)]
        quantize_ky(0)
        weave_ky(1)

        for c in range(2):
            nc.tensor.transpose(bias_ps[:, c, :], bias_pairs[:, c : c + 1].to_broadcast([P, P]), ident[:])
        nc.scalar.copy(out=bias[:].rearrange("p (n c) -> p n c", c=2), in_=bias_ps[:].rearrange("p c n -> p n c"))

        a0_ps = [ps.tile([P, I], F32, name=f"a0_ps{r}", tag=f"bank{r}") for r in range(ROW_TILES)]
        gather(pick_w[0][:], xt_w[0][:], U32, whole_list)
        ky_w.append(sb.tile([P, I], U32, name="ky_w1", tag="xt_w0", align_bytes=64))
        quantize_ky(1)
        for r in range(ROW_TILES):
            score_pass(0, r)

        for r in range(ROW_TILES):
            gather(pick_w[1][:, r * P : (r + 1) * P], xt_w[1][:], U32, slice(r * LIST_COLS, (r + 1) * LIST_COLS))
            score_pass(1, r)

        for r in range(ROW_TILES):
            nc.tensor.matmul_mx(
                out=q_ps[r][:],
                lhsT=cx_w[:, r * P // 2 : (r + 1) * P // 2].bitcast(E2M1),
                lhsT_scale=cx_s[:].bitcast(U8)[:, r * P : (r + 1) * P],
                rhs=wc_w[:].bitcast(E4M3),
                rhs_scale=wc_s[:].bitcast(U8),
                start=True,
                stop=True,
            )

        for r in range(ROW_TILES):
            nc.vector.tensor_tensor(score[r][:], a0_ps[r][:], bias[:], ALU.add)
        for r in range(ROW_TILES):
            nc.vector.tensor_tensor(diff[r][:], q_ps[r][:], score[r][:], ALU.subtract)
        for r in range(ROW_TILES):
            nc.vector.scalar_tensor_tensor(kept[r][:], diff[r][:], -0.5, diff[r][:], ALU.mult, ALU.max)
        for r in range(ROW_TILES):
            nc.vector.scalar_tensor_tensor(res[r][:], score[r][:], 0.5, kept[r][:], ALU.mult, ALU.add)
            (nc.sync, nc.scalar)[r].dma_start(out=out[r * P : (r + 1) * P, :], in_=res[r][:])
